import numpy as np
import ml_dtypes


def mxq(x, axis, fmt="e4m3"):
    dtype, down = {"e4m3": (ml_dtypes.float8_e4m3fn, 7), "e5m2": (ml_dtypes.float8_e5m2, 14)}[fmt]
    v = np.moveaxis(np.asarray(x, np.float32).astype(ml_dtypes.bfloat16).astype(np.float64), axis, -1)
    blocks = v.reshape(v.shape[:-1] + (-1, 32))
    amax = np.abs(blocks).max(-1, keepdims=True)
    byte = np.maximum(np.where(amax > 0, np.frexp(amax)[1] - 1 + 127, 0) - down, 1)
    scale = np.exp2(byte - 127.0)
    codes = (blocks / scale).astype(np.float32).astype(dtype).astype(np.float64)
    return np.moveaxis((codes * scale).reshape(v.shape), -1, axis)


WIDE = False


def mx_kscale(k):
    if not WIDE:
        return np.ones(k)
    levels = np.array([10, -10, 5, -5, 0])
    if k % 512:
        return np.exp2(np.random.permutation(np.resize(levels, k // 32))).repeat(32)
    a = np.empty((k // 512, 16))
    for p in range(k // 512):
        a[p, :8] = np.random.permutation(np.resize(levels, 8))
        for g in range(8):
            far = levels[np.abs(levels - a[p, g]) >= 10]
            a[p, g + 8] = far[np.random.randint(len(far))]
    return np.exp2(a.ravel()).repeat(32)


def f64(x):
    return np.asarray(x).astype(np.float64)


def striped(idx):
    return np.tile(np.asarray(idx).reshape(-1, 16).T, (8, 1)).astype(np.uint16)


def unstriped(offs):
    return offs[:16].T.reshape(-1).astype(np.int64)


E2M1 = np.array([0.0, 0.5, 1.0, 1.5, 2.0, 3.0, 4.0, 6.0, -0.0, -0.5, -1.0, -1.5, -2.0, -3.0, -4.0, -6.0])


def pack_weight(w, fmt):
    k, n = w.shape
    w = f64(np.asarray(w, np.float32).astype(ml_dtypes.bfloat16)).reshape(k // 32, 32, n)
    amax = np.abs(w).max(1)
    if fmt == "e4m3":
        byte = np.frexp(amax)[1] - 1 + 127 - 7
    else:
        mant, ex = np.frexp(amax / 6.0)
        byte = np.where(mant > 0.5, ex, ex - 1) + 127
    byte = np.clip(np.where(amax > 0, byte, 1), 1, 254)
    scaled = (w * np.exp2(127.0 - byte)[:, None, :]).reshape(k, n).astype(np.float32)
    by_word = np.ascontiguousarray(scaled.reshape(k // 512, 128, 4, n).transpose(0, 1, 3, 2))
    if fmt == "e4m3":
        words = by_word.astype(ml_dtypes.float8_e4m3fn).view(np.uint8)
    else:
        c = by_word.astype(ml_dtypes.float4_e2m1fn).view(np.uint8) & 0xF
        words = (c[..., 0::2] | (c[..., 1::2] << 4)).reshape(k // 512, 128, 2 * n)
    return np.ascontiguousarray(words), np.ascontiguousarray(byte.astype(np.uint8).reshape(k // 512, 16, n))


def unpack_weight(words, scales, fmt):
    g, _, n = scales.shape
    words = np.ascontiguousarray(words).reshape(g, 128, n, -1)
    if fmt == "e4m3":
        vals = words.view(ml_dtypes.float8_e4m3fn).astype(np.float64)
    else:
        nib = np.empty((g, 128, n, 4), np.uint8)
        nib[..., 0::2] = words & 0xF
        nib[..., 1::2] = words >> 4
        vals = E2M1[nib]
    vals = vals * np.repeat(np.exp2(scales.astype(np.float64) - 127.0), 8, axis=1)[..., None]
    return vals.transpose(0, 1, 3, 2).reshape(g * 512, n)


K, T, J, N = 1024, 2048, 512, 512


def setup_inputs():
    n = np.random.standard_normal
    idx = np.random.permutation(T)[:J]
    fk = mx_kscale(K)
    xtp = pack_weight(n((K, T)) / fk[:, None], "e4m3")
    wbp = pack_weight(n((K, N)) * 1 / np.sqrt(K) * fk[:, None], "e2m1")
    return {
        "xt_words": xtp[0],
        "xt_scales": xtp[1],
        "wa": (n((K, N)) * 1 / np.sqrt(K) * fk[:, None]).astype(np.float32),
        "wb_words": wbp[0],
        "wb_scales": wbp[1],
        "ga": (np.random.uniform(0.4, 1.2, (1, J))).astype(np.float32),
        "offs": striped(idx),
    }


def reference(xt_words, xt_scales, wa, wb_words, wb_scales, ga, offs):
    idx = unstriped(offs)
    xtu = unpack_weight(xt_words, xt_scales, "e4m3")
    wbu = unpack_weight(wb_words, wb_scales, "e2m1")
    waq = mxq(f64(wa), 0, "e4m3")
    xtidxg = xtu[:, idx]
    a = waq.T @ xtidxg
    b = wbu.T @ xtidxg
    ea = np.exp(0.5 * a)
    eb = np.exp(0.5 * b)
    y = f64(ga) * (ea * a + eb * b) / (ea + eb)
    return y

@@ -1,0 +1,153 @@
+from contextlib import ExitStack
+
+import concourse.mybir as mybir
+from concourse.masks import make_identity
+
+F32 = mybir.dt.float32
+BF16 = mybir.dt.bfloat16
+I32 = mybir.dt.int32
+U32 = mybir.dt.uint32
+U16 = mybir.dt.uint16
+U8 = mybir.dt.uint8
+FP8X4 = mybir.dt.float8_e4m3fn_x4
+FP4X4 = mybir.dt.float4_e2m1fn_x4
+ALU = mybir.AluOpType
+ACT = mybir.ActivationFunctionType
+
+P = 128
+K, T, J, N = 1024, 2048, 512, 512
+PASSES = 2
+TILES = 4
+SPLIT_TILES = 2
+FLOPS = 2 * 2 * K * N * J
+
+
+def tile_moe_soft_larger_of_two_experts_kernel(tc, xt_words, xt_scales, wa, wb_words, wb_scales, ga, offs, out):
+    nc = tc.nc
+    with ExitStack() as ctx:
+        sb = ctx.enter_context(tc.tile_pool(name="sb", bufs=1))
+        ps = ctx.enter_context(tc.psum_pool(name="ps", bufs=1))
+
+        offsets = sb.tile([P, J // 16], U16, name="offsets")
+        x_scale_win = sb.tile([P, PASSES, T], U8, name="x_scale_win", align_bytes=64)
+        wb_scale = sb.tile([P, PASSES, N], U8, name="wb_scale", align_bytes=64)
+        wb_code = sb.tile([P, PASSES, 2 * N], U8, name="wb_code", align_bytes=64)
+        x_win = [sb.tile([P, T], U32, name="x_win0", tag="early_x", align_bytes=64)]
+        ga_col = sb.tile([P, 4], F32, name="ga_col")
+        ident = sb.tile([P, P], F32, name="ident")
+        warm = sb.tile([P, 8], F32, name="warm")
+        warm_out = sb.tile([P, 8], F32, name="warm_out")
+
+        nc.vector.memset(x_scale_win[:].bitcast(I32), 0)
+        nc.vector.memset(warm[:], 0.0)
+        nc.gpsimd.memset(wb_scale[:].bitcast(I32), 0)
+
+        def load_scales(eng, plane, rows):
+            src = rows.bitcast(I32).rearrange("z (Q r) c -> r Q z c", r=4)
+            for r in range(4):
+                eng.dma_start(plane[:].bitcast(I32)[r:P:32, :, :], src[r])
+
+        def load_words(z):
+            nc.sync.dma_start(x_win[z][:].bitcast(I32), xt_words[z].rearrange("p c r -> p (c r)").bitcast(I32))
+
+        wa_rows = wa.rearrange("(z p r) n -> z p r n", z=PASSES, r=4)
+
+        nc.sync.dma_start(offsets[:], offs)
+        load_words(0)
+        load_scales(nc.scalar, x_scale_win, xt_scales)
+        nc.sync.dma_start(wb_code[:].bitcast(I32), wb_words.rearrange("z p c -> p z c").bitcast(I32))
+        load_scales(nc.gpsimd, wb_scale, wb_scales)
+        nc.gpsimd.dma_start(ga_col[:], ga.rearrange("o (p c) -> p (o c)", c=4))
+        nc.scalar.activation(warm_out[:], warm[:], ACT.Silu)
+        raw0 = sb.tile([P, 4, N], F32, name="raw0", align_bytes=64)
+        nc.sync.dma_start(raw0[:], wa_rows[0])
+        x_win.append(sb.tile([P, T], U32, name="x_win1", align_bytes=64))
+        load_words(1)
+
+        make_identity(nc, ident[:])
+        ga_ps = ps.tile([P, 4, P], F32, name="ga_ps", tag="e3")
+        for c in range(4):
+            nc.tensor.transpose(ga_ps[:, c, :], ga_col[:, c:c + 1].to_broadcast([P, P]), ident[:])
+        ga_all = sb.tile([P, J], F32, name="ga_all")
+        nc.scalar.copy(ga_all[:].rearrange("p (n c) -> p n c", c=4), ga_ps[:].rearrange("p c n -> p n c"))
+
+        x_code = [sb.tile([P, J], U32, name=f"x_code{z}", align_bytes=64) for z in range(PASSES)]
+        x_scale = [sb.tile([P, J], U8, name=f"x_scale{z}", align_bytes=64) for z in range(PASSES)]
+
+        def gather_scales(z):
+            nc.vector.tensor_copy(x_scale[z][:], x_scale_win[:, z, :].indirect(offsets[:]))
+
+        def gather_words(z):
+            nc.vector.tensor_copy(x_code[z][:], x_win[z][:].indirect(offsets[:]))
+
+        wa_q = {}
+
+        def cast(eng, raw, width, name):
+            grouped = sb.tile([P, width, 4], BF16, name="g" + name, align_bytes=64)
+            dst = grouped[:].rearrange("p (c i) r -> p c r i", i=4)
+            src = raw.rearrange("p r (c i) -> p c r i", i=4)
+            if eng is nc.scalar:
+                nc.scalar.activation(dst, src, ACT.Copy, scale=-1.0)
+            else:
+                eng.tensor_scalar(dst, src, -1.0, 0.0, ALU.mult, ALU.add)
+            return grouped
+
+        def quantise(grouped, width, name, z, m0):
+            code = sb.tile([P, width], U32, name="c" + name, align_bytes=64)
+            scale = sb.tile([P, width], U8, name="s" + name, align_bytes=64)
+            nc.vector.quantize_mx(code[:].bitcast(FP8X4), scale[:], grouped[:].rearrange("p n r -> p (n r)"))
+            for i in range(width // P):
+                wa_q[(z, m0 + i)] = (code[:, i * P:(i + 1) * P], scale[:, i * P:(i + 1) * P])
+
+        b_ps = [ps.tile([P, J], F32, name=f"b{m}", tag=f"b{m}") for m in range(TILES)]
+        e_ps = [ps.tile([P, J], F32, name=f"e{m}", tag=f"e{m}") for m in range(TILES)]
+
+        def mm_b(dst, z, m, start, stop):
+            nc.tensor.matmul_mx(dst[:], lhsT=wb_code[:, z, 2 * m * P:2 * (m + 1) * P].bitcast(FP4X4),
+                                lhsT_scale=wb_scale[:, z, m * P:(m + 1) * P],
+                                rhs=x_code[z][:].bitcast(FP8X4), rhs_scale=x_scale[z][:], start=start, stop=stop)
+
+        def mm_a(z, m, start, stop):
+            code, scale = wa_q[(z, m)]
+            nc.tensor.matmul_mx(e_ps[m][:], lhsT=code.bitcast(FP8X4), lhsT_scale=scale,
+                                rhs=x_code[z][:].bitcast(FP8X4), rhs_scale=x_scale[z][:], start=start, stop=stop)
+
+        gather_words(0)
+        gather_scales(0)
+        gather_scales(1)
+        raw1 = sb.tile([P, TILES, 4, P], F32, name="raw1", tag="early_x", align_bytes=64)
+        for m in range(TILES):
+            nc.sync.dma_start(raw1[:, m, :, :], wa_rows[1][:, :, m * P:(m + 1) * P])
+        for m in range(TILES):
+            mm_b(b_ps[m], 0, m, True, False)
+        for m in range(SPLIT_TILES, TILES):
+            mm_b(e_ps[m], 0, m, True, False)
+        for h in range(2):
+            g = cast(nc.scalar, raw0[:, :, h * 256:(h + 1) * 256], 256, f"0_{h}")
+            quantise(g, 256, f"0_{h}", 0, 2 * h)
+            for m in range(2 * h, 2 * h + 2):
+                mm_a(0, m, m < SPLIT_TILES, False)
+        gather_words(1)
+
+        for m in range(TILES):
+            g = cast(nc.scalar if m % 2 == 0 else nc.vector, raw1[:, m, :, :], P, f"1_{m}")
+            quantise(g, P, f"1_{m}", 1, m)
+            mm_b(b_ps[m], 1, m, False, True)
+            if m >= SPLIT_TILES:
+                mm_b(e_ps[m], 1, m, False, False)
+            mm_a(1, m, False, True)
+            s = sb.tile([P, J], F32, name=f"s{m}")
+            if m < SPLIT_TILES:
+                b_sb = sb.tile([P, J], F32, name=f"b_sb{m}")
+                nc.scalar.copy(b_sb[:], b_ps[m][:])
+                e_sb = sb.tile([P, J], F32, name=f"e_sb{m}")
+                nc.vector.tensor_tensor(e_sb[:], e_ps[m][:], b_sb[:], ALU.add)
+                nc.scalar.activation(s[:], e_sb[:], ACT.Silu, scale=-0.5)
+            else:
+                nc.scalar.activation(s[:], e_ps[m][:], ACT.Silu, scale=-0.5)
+            t = sb.tile([P, J], F32, name=f"t{m}")
+            nc.vector.scalar_tensor_tensor(t[:], s[:], 2.0, b_ps[m][:], ALU.mult, ALU.add)
+            y = sb.tile([P, J], F32, name=f"y{m}")
+            eng = nc.vector if m == TILES - 1 else nc.gpsimd
+            eng.tensor_tensor(y[:], t[:], ga_all[:], ALU.mult)
+            nc.sync.dma_start(out[m * P:(m + 1) * P, :], y[:])

@@ -30,17 +30,17 @@ def tile_moe_soft_larger_of_two_experts_kernel(tc, xt_words, xt_scales, wa, wb_w
 
         offsets = sb.tile([P, J // 16], U16, name="offsets")
         x_scale_win = sb.tile([P, PASSES, T], U8, name="x_scale_win", align_bytes=64)
-        wb_scale = sb.tile([P, PASSES, N], U8, name="wb_scale", align_bytes=64)
         wb_code = sb.tile([P, PASSES, 2 * N], U8, name="wb_code", align_bytes=64)
         x_win = [sb.tile([P, T], U32, name="x_win0", tag="early_x", align_bytes=64)]
-        ga_col = sb.tile([P, 4], F32, name="ga_col")
+        ga_col = sb.tile([P, 4], F32, name="ga_col", tag="then_wa", align_bytes=64)
         ident = sb.tile([P, P], F32, name="ident")
-        warm = sb.tile([P, 8], F32, name="warm")
-        warm_out = sb.tile([P, 8], F32, name="warm_out")
+        warm = sb.tile([P, 8], F32, name="warm", tag="then_x1", align_bytes=64)
+        warm_out = sb.tile([P, 8], F32, name="warm_out", tag="then_wbs", align_bytes=64)
 
+        nc.gpsimd.memset(warm[:], 0.0)
         nc.vector.memset(x_scale_win[:].bitcast(I32), 0)
-        nc.vector.memset(warm[:], 0.0)
-        nc.gpsimd.memset(wb_scale[:].bitcast(I32), 0)
+        make_identity(nc, ident[:])
+        nc.scalar.activation(warm_out[:], warm[:], ACT.Silu)
 
         def load_scales(eng, plane, rows):
             src = rows.bitcast(I32).rearrange("z (Q r) c -> r Q z c", r=4)
@@ -53,21 +53,22 @@ def tile_moe_soft_larger_of_two_experts_kernel(tc, xt_words, xt_scales, wa, wb_w
         wa_rows = wa.rearrange("(z p r) n -> z p r n", z=PASSES, r=4)
 
         nc.sync.dma_start(offsets[:], offs)
+        nc.sync.dma_start(ga_col[:], ga.rearrange("o (p c) -> p (o c)", c=4))
         load_words(0)
-        load_scales(nc.scalar, x_scale_win, xt_scales)
+        load_scales(nc.sync, x_scale_win, xt_scales)
         nc.sync.dma_start(wb_code[:].bitcast(I32), wb_words.rearrange("z p c -> p z c").bitcast(I32))
-        load_scales(nc.gpsimd, wb_scale, wb_scales)
-        nc.gpsimd.dma_start(ga_col[:], ga.rearrange("o (p c) -> p (o c)", c=4))
-        nc.scalar.activation(warm_out[:], warm[:], ACT.Silu)
-        raw0 = sb.tile([P, 4, N], F32, name="raw0", align_bytes=64)
-        nc.sync.dma_start(raw0[:], wa_rows[0])
-        x_win.append(sb.tile([P, T], U32, name="x_win1", align_bytes=64))
+        x_win.append(sb.tile([P, T], U32, name="x_win1", tag="then_x1", align_bytes=64))
         load_words(1)
+        wb_scale = sb.tile([P, PASSES, N], U8, name="wb_scale", tag="then_wbs", align_bytes=64)
+        nc.gpsimd.memset(wb_scale[:].bitcast(I32), 0)
+        load_scales(nc.scalar, wb_scale, wb_scales)
 
-        make_identity(nc, ident[:])
         ga_ps = ps.tile([P, 4, P], F32, name="ga_ps", tag="e3")
         for c in range(4):
             nc.tensor.transpose(ga_ps[:, c, :], ga_col[:, c:c + 1].to_broadcast([P, P]), ident[:])
+        raw_first = sb.tile([P, 4 * 256], F32, name="raw_first", tag="then_wa", align_bytes=64)
+        raw = {"A0": raw_first[:].rearrange("p (r n) -> p r n", r=4)}
+        nc.sync.dma_start(raw["A0"], wa_rows[0][:, :, 0:256])
         ga_all = sb.tile([P, J], F32, name="ga_all")
         nc.scalar.copy(ga_all[:].rearrange("p (n c) -> p n c", c=4), ga_ps[:].rearrange("p c n -> p n c"))
 
@@ -114,40 +115,78 @@ def tile_moe_soft_larger_of_two_experts_kernel(tc, xt_words, xt_scales, wa, wb_w
 
         gather_words(0)
         gather_scales(0)
+        raw_rest = sb.tile([P, 4 * 768], F32, name="raw_rest", tag="early_x", align_bytes=64)
+        at = 0
+        for name, z, c0, width in (("A1", 1, 0, 256), ("B0", 0, 256, 256), ("C1", 1, 256, 128), ("D1", 1, 384, 128)):
+            raw[name] = raw_rest[:, at:at + 4 * width].rearrange("p (r n) -> p r n", r=4)
+            nc.sync.dma_start(raw[name], wa_rows[z][:, :, c0:c0 + width])
+            at = at + 4 * width
         gather_scales(1)
-        raw1 = sb.tile([P, TILES, 4, P], F32, name="raw1", tag="early_x", align_bytes=64)
-        for m in range(TILES):
-            nc.sync.dma_start(raw1[:, m, :, :], wa_rows[1][:, :, m * P:(m + 1) * P])
         for m in range(TILES):
             mm_b(b_ps[m], 0, m, True, False)
         for m in range(SPLIT_TILES, TILES):
             mm_b(e_ps[m], 0, m, True, False)
-        for h in range(2):
-            g = cast(nc.scalar, raw0[:, :, h * 256:(h + 1) * 256], 256, f"0_{h}")
-            quantise(g, 256, f"0_{h}", 0, 2 * h)
-            for m in range(2 * h, 2 * h + 2):
-                mm_a(0, m, m < SPLIT_TILES, False)
         gather_words(1)
-
-        for m in range(TILES):
-            g = cast(nc.scalar if m % 2 == 0 else nc.vector, raw1[:, m, :, :], P, f"1_{m}")
-            quantise(g, P, f"1_{m}", 1, m)
+        for m in range(SPLIT_TILES):
             mm_b(b_ps[m], 1, m, False, True)
-            if m >= SPLIT_TILES:
-                mm_b(e_ps[m], 1, m, False, False)
+
+        b_sb = [sb.tile([P, J], F32, name=f"b_sb{m}") for m in range(SPLIT_TILES)]
+        e_sb = [sb.tile([P, J], F32, name=f"e_sb{m}") for m in range(SPLIT_TILES)]
+        s = [sb.tile([P, J], F32, name=f"s{m}") for m in range(TILES)]
+        t = [sb.tile([P, J], F32, name=f"t{m}") for m in range(TILES)]
+        y = [sb.tile([P, J], F32, name=f"y{m}") for m in range(TILES)]
+
+        def sub(m):
+            nc.vector.tensor_tensor(e_sb[m][:], e_ps[m][:], b_sb[m][:], ALU.add)
+
+        def silu(m, cols=slice(0, J)):
+            src = e_sb[m] if m < SPLIT_TILES else e_ps[m]
+            nc.scalar.activation(s[m][:, cols], src[:, cols], ACT.Silu, scale=-0.5)
+
+        def blend(m, cols=slice(0, J)):
+            nc.vector.scalar_tensor_tensor(t[m][:, cols], s[m][:, cols], 2.0, b_ps[m][:, cols], ALU.mult, ALU.add)
+
+        def gate(eng, m, cols=slice(0, J)):
+            eng.tensor_tensor(y[m][:, cols], t[m][:, cols], ga_all[:, cols], ALU.mult)
+            nc.sync.dma_start(out[m * P:(m + 1) * P, cols], y[m][:, cols])
+
+        quantise(cast(nc.vector, raw["A0"], 256, "A0"), 256, "A0", 0, 0)
+        for m in range(SPLIT_TILES):
+            nc.vector.tensor_copy(b_sb[m][:], b_ps[m][:])
+        g_a1 = cast(nc.scalar, raw["A1"], 256, "A1")
+        for m in range(SPLIT_TILES):
+            mm_a(0, m, True, False)
+        quantise(g_a1, 256, "A1", 1, 0)
+        for m in range(SPLIT_TILES):
             mm_a(1, m, False, True)
-            s = sb.tile([P, J], F32, name=f"s{m}")
-            if m < SPLIT_TILES:
-                b_sb = sb.tile([P, J], F32, name=f"b_sb{m}")
-                nc.scalar.copy(b_sb[:], b_ps[m][:])
-                e_sb = sb.tile([P, J], F32, name=f"e_sb{m}")
-                nc.vector.tensor_tensor(e_sb[:], e_ps[m][:], b_sb[:], ALU.add)
-                nc.scalar.activation(s[:], e_sb[:], ACT.Silu, scale=-0.5)
-            else:
-                nc.scalar.activation(s[:], e_ps[m][:], ACT.Silu, scale=-0.5)
-            t = sb.tile([P, J], F32, name=f"t{m}")
-            nc.vector.scalar_tensor_tensor(t[:], s[:], 2.0, b_ps[m][:], ALU.mult, ALU.add)
-            y = sb.tile([P, J], F32, name=f"y{m}")
-            eng = nc.vector if m == TILES - 1 else nc.gpsimd
-            eng.tensor_tensor(y[:], t[:], ga_all[:], ALU.mult)
-            nc.sync.dma_start(out[m * P:(m + 1) * P, :], y[:])
+        for m in range(SPLIT_TILES, TILES):
+            mm_b(b_ps[m], 1, m, False, True)
+            mm_b(e_ps[m], 1, m, False, False)
+        g_b0 = cast(nc.scalar, raw["B0"], 256, "B0")
+        sub(0)
+        g_c1 = cast(nc.scalar, raw["C1"], 128, "C1")
+        quantise(g_b0, 256, "B0", 0, 2)
+        sub(1)
+        silu(0)
+        for m in range(SPLIT_TILES, TILES):
+            mm_a(0, m, False, False)
+        quantise(g_c1, 128, "C1", 1, 2)
+        mm_a(1, 2, False, True)
+        g_d1 = cast(nc.scalar, raw["D1"], 128, "D1")
+        blend(0)
+        quantise(g_d1, 128, "D1", 1, 3)
+        mm_a(1, 3, False, True)
+        gate(nc.gpsimd, 0)
+        silu(1)
+        blend(1)
+        gate(nc.gpsimd, 1)
+        silu(2)
+        blend(2)
+        halves = (slice(0, J // 2), slice(J // 2, J))
+        for cols in halves:
+            silu(3, cols)
+        gate(nc.vector, 2)
+        for cols in halves:
+            blend(3, cols)
+        for cols in halves:
+            gate(nc.vector, 3, cols)

@@ -30,22 +30,23 @@ def tile_moe_soft_larger_of_two_experts_kernel(tc, xt_words, xt_scales, wa, wb_w
 
         offsets = sb.tile([P, J // 16], U16, name="offsets")
         x_scale_win = sb.tile([P, PASSES, T], U8, name="x_scale_win", align_bytes=64)
-        wb_code = sb.tile([P, PASSES, 2 * N], U8, name="wb_code", align_bytes=64)
         x_win = [sb.tile([P, T], U32, name="x_win0", tag="early_x", align_bytes=64)]
         ga_col = sb.tile([P, 4], F32, name="ga_col", tag="then_wa", align_bytes=64)
         ident = sb.tile([P, P], F32, name="ident")
         warm = sb.tile([P, 8], F32, name="warm", tag="then_x1", align_bytes=64)
-        warm_out = sb.tile([P, 8], F32, name="warm_out", tag="then_wbs", align_bytes=64)
+        warm_out = sb.tile([P, 8], F32, name="warm_out", tag="then_wb", align_bytes=64)
 
         nc.gpsimd.memset(warm[:], 0.0)
         nc.vector.memset(x_scale_win[:].bitcast(I32), 0)
         make_identity(nc, ident[:])
+        wb_scale = sb.tile([P, PASSES, N], U8, name="wb_scale", align_bytes=64)
+        nc.gpsimd.memset(wb_scale[:].bitcast(I32), 0)
         nc.scalar.activation(warm_out[:], warm[:], ACT.Silu)
 
         def load_scales(eng, plane, rows):
             src = rows.bitcast(I32).rearrange("z (Q r) c -> r Q z c", r=4)
             for r in range(4):
-                eng.dma_start(plane[:].bitcast(I32)[r:P:32, :, :], src[r])
+                eng[r].dma_start(plane[:].bitcast(I32)[r:P:32, :, :], src[r])
 
         def load_words(z):
             nc.sync.dma_start(x_win[z][:].bitcast(I32), xt_words[z].rearrange("p c r -> p (c r)").bitcast(I32))
@@ -55,13 +56,12 @@ def tile_moe_soft_larger_of_two_experts_kernel(tc, xt_words, xt_scales, wa, wb_w
         nc.sync.dma_start(offsets[:], offs)
         nc.sync.dma_start(ga_col[:], ga.rearrange("o (p c) -> p (o c)", c=4))
         load_words(0)
-        load_scales(nc.sync, x_scale_win, xt_scales)
+        load_scales([nc.sync] * 4, x_scale_win, xt_scales)
+        wb_code = sb.tile([P, PASSES, 2 * N], U8, name="wb_code", tag="then_wb", align_bytes=64)
         nc.sync.dma_start(wb_code[:].bitcast(I32), wb_words.rearrange("z p c -> p z c").bitcast(I32))
         x_win.append(sb.tile([P, T], U32, name="x_win1", tag="then_x1", align_bytes=64))
         load_words(1)
-        wb_scale = sb.tile([P, PASSES, N], U8, name="wb_scale", tag="then_wbs", align_bytes=64)
-        nc.gpsimd.memset(wb_scale[:].bitcast(I32), 0)
-        load_scales(nc.scalar, wb_scale, wb_scales)
+        load_scales([nc.sync, nc.gpsimd, nc.gpsimd, nc.gpsimd], wb_scale, wb_scales)
 
         ga_ps = ps.tile([P, 4, P], F32, name="ga_ps", tag="e3")
         for c in range(4):
@@ -150,33 +150,33 @@ def tile_moe_soft_larger_of_two_experts_kernel(tc, xt_words, xt_scales, wa, wb_w
             eng.tensor_tensor(y[m][:, cols], t[m][:, cols], ga_all[:, cols], ALU.mult)
             nc.sync.dma_start(out[m * P:(m + 1) * P, cols], y[m][:, cols])
 
-        quantise(cast(nc.vector, raw["A0"], 256, "A0"), 256, "A0", 0, 0)
-        for m in range(SPLIT_TILES):
-            nc.vector.tensor_copy(b_sb[m][:], b_ps[m][:])
-        g_a1 = cast(nc.scalar, raw["A1"], 256, "A1")
+        quantise(cast(nc.scalar, raw["A0"], 256, "A0"), 256, "A0", 0, 0)
         for m in range(SPLIT_TILES):
             mm_a(0, m, True, False)
+        g_a1 = cast(nc.scalar, raw["A1"], 256, "A1")
+        for m in range(SPLIT_TILES):
+            nc.vector.tensor_copy(b_sb[m][:], b_ps[m][:])
         quantise(g_a1, 256, "A1", 1, 0)
         for m in range(SPLIT_TILES):
             mm_a(1, m, False, True)
         for m in range(SPLIT_TILES, TILES):
-            mm_b(b_ps[m], 1, m, False, True)
             mm_b(e_ps[m], 1, m, False, False)
+            mm_b(b_ps[m], 1, m, False, True)
         g_b0 = cast(nc.scalar, raw["B0"], 256, "B0")
         sub(0)
-        g_c1 = cast(nc.scalar, raw["C1"], 128, "C1")
         quantise(g_b0, 256, "B0", 0, 2)
-        sub(1)
-        silu(0)
         for m in range(SPLIT_TILES, TILES):
             mm_a(0, m, False, False)
+        sub(1)
+        g_c1 = cast(nc.scalar, raw["C1"], 128, "C1")
+        silu(0)
+        g_d1 = cast(nc.scalar, raw["D1"], 128, "D1")
         quantise(g_c1, 128, "C1", 1, 2)
         mm_a(1, 2, False, True)
-        g_d1 = cast(nc.scalar, raw["D1"], 128, "D1")
         blend(0)
+        gate(nc.gpsimd, 0)
         quantise(g_d1, 128, "D1", 1, 3)
         mm_a(1, 3, False, True)
-        gate(nc.gpsimd, 0)
         silu(1)
         blend(1)
         gate(nc.gpsimd, 1)

@@ -26,19 +26,19 @@ def tile_moe_soft_larger_of_two_experts_kernel(tc, xt_words, xt_scales, wa, wb_w
     nc = tc.nc
     with ExitStack() as ctx:
         sb = ctx.enter_context(tc.tile_pool(name="sb", bufs=1))
+        shared = ctx.enter_context(tc.tile_pool(name="shared", bufs=1))
         ps = ctx.enter_context(tc.psum_pool(name="ps", bufs=1))
 
         offsets = sb.tile([P, J // 16], U16, name="offsets")
         x_scale_win = sb.tile([P, PASSES, T], U8, name="x_scale_win", align_bytes=64)
-        x_win = [sb.tile([P, T], U32, name="x_win0", tag="early_x", align_bytes=64)]
-        ga_col = sb.tile([P, 4], F32, name="ga_col", tag="then_wa", align_bytes=64)
+        x_win = [shared.tile([P, T], U32, name="x_win0", offset=0, align_bytes=64)]
+        ga_col = sb.tile([P, 4], F32, name="ga_col")
         ident = sb.tile([P, P], F32, name="ident")
         warm = sb.tile([P, 8], F32, name="warm", tag="then_x1", align_bytes=64)
         warm_out = sb.tile([P, 8], F32, name="warm_out", tag="then_wb", align_bytes=64)
 
         nc.gpsimd.memset(warm[:], 0.0)
         nc.vector.memset(x_scale_win[:].bitcast(I32), 0)
-        make_identity(nc, ident[:])
         wb_scale = sb.tile([P, PASSES, N], U8, name="wb_scale", align_bytes=64)
         nc.gpsimd.memset(wb_scale[:].bitcast(I32), 0)
         nc.scalar.activation(warm_out[:], warm[:], ACT.Silu)
@@ -63,17 +63,21 @@ def tile_moe_soft_larger_of_two_experts_kernel(tc, xt_words, xt_scales, wa, wb_w
         load_words(1)
         load_scales([nc.sync, nc.gpsimd, nc.gpsimd, nc.gpsimd], wb_scale, wb_scales)
 
+        make_identity(nc, ident[:])
         ga_ps = ps.tile([P, 4, P], F32, name="ga_ps", tag="e3")
         for c in range(4):
             nc.tensor.transpose(ga_ps[:, c, :], ga_col[:, c:c + 1].to_broadcast([P, P]), ident[:])
-        raw_first = sb.tile([P, 4 * 256], F32, name="raw_first", tag="then_wa", align_bytes=64)
-        raw = {"A0": raw_first[:].rearrange("p (r n) -> p r n", r=4)}
-        nc.sync.dma_start(raw["A0"], wa_rows[0][:, :, 0:256])
+        raw = {}
+
+        def load_wa(tile, at, z, m):
+            raw[(z, m)] = tile[:, at * 4 * P:(at + 1) * 4 * P].rearrange("p (r n) -> p r n", r=4)
+            nc.sync.dma_start(raw[(z, m)], wa_rows[z][:, :, m * P:(m + 1) * P])
+
         ga_all = sb.tile([P, J], F32, name="ga_all")
         nc.scalar.copy(ga_all[:].rearrange("p (n c) -> p n c", c=4), ga_ps[:].rearrange("p c n -> p n c"))
 
         x_code = [sb.tile([P, J], U32, name=f"x_code{z}", align_bytes=64) for z in range(PASSES)]
-        x_scale = [sb.tile([P, J], U8, name=f"x_scale{z}", align_bytes=64) for z in range(PASSES)]
+        x_scale = [shared.tile([P, J], U8, name=f"x_scale{z}", offset=z * J, align_bytes=64) for z in range(PASSES)]
 
         def gather_scales(z):
             nc.vector.tensor_copy(x_scale[z][:], x_scale_win[:, z, :].indirect(offsets[:]))
@@ -115,20 +119,16 @@ def tile_moe_soft_larger_of_two_experts_kernel(tc, xt_words, xt_scales, wa, wb_w
 
         gather_words(0)
         gather_scales(0)
-        raw_rest = sb.tile([P, 4 * 768], F32, name="raw_rest", tag="early_x", align_bytes=64)
-        at = 0
-        for name, z, c0, width in (("A1", 1, 0, 256), ("B0", 0, 256, 256), ("C1", 1, 256, 128), ("D1", 1, 384, 128)):
-            raw[name] = raw_rest[:, at:at + 4 * width].rearrange("p (r n) -> p r n", r=4)
-            nc.sync.dma_start(raw[name], wa_rows[z][:, :, c0:c0 + width])
-            at = at + 4 * width
+        raw_rest = shared.tile([P, 4 * 1024], F32, name="raw_rest", offset=PASSES * J, align_bytes=64)
+        for m in range(TILES):
+            for z in range(PASSES):
+                load_wa(raw_rest, PASSES * m + z, z, m)
         gather_scales(1)
         for m in range(TILES):
+            if m >= SPLIT_TILES:
+                mm_b(e_ps[m], 0, m, True, False)
             mm_b(b_ps[m], 0, m, True, False)
-        for m in range(SPLIT_TILES, TILES):
-            mm_b(e_ps[m], 0, m, True, False)
         gather_words(1)
-        for m in range(SPLIT_TILES):
-            mm_b(b_ps[m], 1, m, False, True)
 
         b_sb = [sb.tile([P, J], F32, name=f"b_sb{m}") for m in range(SPLIT_TILES)]
         e_sb = [sb.tile([P, J], F32, name=f"e_sb{m}") for m in range(SPLIT_TILES)]
@@ -150,43 +150,30 @@ def tile_moe_soft_larger_of_two_experts_kernel(tc, xt_words, xt_scales, wa, wb_w
             eng.tensor_tensor(y[m][:, cols], t[m][:, cols], ga_all[:, cols], ALU.mult)
             nc.sync.dma_start(out[m * P:(m + 1) * P, cols], y[m][:, cols])
 
-        quantise(cast(nc.scalar, raw["A0"], 256, "A0"), 256, "A0", 0, 0)
-        for m in range(SPLIT_TILES):
-            mm_a(0, m, True, False)
-        g_a1 = cast(nc.scalar, raw["A1"], 256, "A1")
-        for m in range(SPLIT_TILES):
-            nc.vector.tensor_copy(b_sb[m][:], b_ps[m][:])
-        quantise(g_a1, 256, "A1", 1, 0)
-        for m in range(SPLIT_TILES):
-            mm_a(1, m, False, True)
-        for m in range(SPLIT_TILES, TILES):
-            mm_b(e_ps[m], 1, m, False, False)
+        def products(m):
+            if m >= SPLIT_TILES:
+                mm_b(e_ps[m], 1, m, False, False)
             mm_b(b_ps[m], 1, m, False, True)
-        g_b0 = cast(nc.scalar, raw["B0"], 256, "B0")
-        sub(0)
-        quantise(g_b0, 256, "B0", 0, 2)
-        for m in range(SPLIT_TILES, TILES):
-            mm_a(0, m, False, False)
-        sub(1)
-        g_c1 = cast(nc.scalar, raw["C1"], 128, "C1")
-        silu(0)
-        g_d1 = cast(nc.scalar, raw["D1"], 128, "D1")
-        quantise(g_c1, 128, "C1", 1, 2)
-        mm_a(1, 2, False, True)
-        blend(0)
-        gate(nc.gpsimd, 0)
-        quantise(g_d1, 128, "D1", 1, 3)
-        mm_a(1, 3, False, True)
-        silu(1)
-        blend(1)
-        gate(nc.gpsimd, 1)
-        silu(2)
-        blend(2)
-        halves = (slice(0, J // 2), slice(J // 2, J))
-        for cols in halves:
-            silu(3, cols)
-        gate(nc.vector, 2)
-        for cols in halves:
-            blend(3, cols)
-        for cols in halves:
-            gate(nc.vector, 3, cols)
+            for z, eng in enumerate((nc.scalar, nc.vector)):
+                quantise(cast(eng, raw[(z, m)], P, f"{z}_{m}"), P, f"{z}_{m}", z, m)
+            for z in range(PASSES):
+                mm_a(z, m, z == 0 and m < SPLIT_TILES, z == 1)
+            if m < SPLIT_TILES:
+                nc.scalar.copy(b_sb[m][:], b_ps[m][:])
+
+        def finish(m):
+            pieces = (slice(0, J // 2), slice(J // 2, J)) if m == TILES - 1 else (slice(0, J),)
+            if m < SPLIT_TILES:
+                sub(m)
+            for cols in pieces:
+                silu(m, cols)
+            for cols in pieces:
+                blend(m, cols)
+            for cols in pieces:
+                gate(nc.gpsimd if m < SPLIT_TILES else nc.vector, m, cols)
+
+        for step in range(TILES + 1):
+            if step < TILES:
+                products(step)
+            if step >= 1:
+                finish(step - 1)

from contextlib import ExitStack

import concourse.mybir as mybir
from concourse.masks import make_identity

F32 = mybir.dt.float32
BF16 = mybir.dt.bfloat16
I32 = mybir.dt.int32
U32 = mybir.dt.uint32
U16 = mybir.dt.uint16
U8 = mybir.dt.uint8
FP8X4 = mybir.dt.float8_e4m3fn_x4
FP4X4 = mybir.dt.float4_e2m1fn_x4
ALU = mybir.AluOpType
ACT = mybir.ActivationFunctionType

P = 128
K, T, J, N = 1024, 2048, 512, 512
PASSES = 2
TILES = 4
SPLIT_TILES = 2
FLOPS = 2 * 2 * K * N * J


def tile_moe_soft_larger_of_two_experts_kernel(tc, xt_words, xt_scales, wa, wb_words, wb_scales, ga, offs, out):
    nc = tc.nc
    with ExitStack() as ctx:
        sb = ctx.enter_context(tc.tile_pool(name="sb", bufs=1))
        shared = ctx.enter_context(tc.tile_pool(name="shared", bufs=1))
        ps = ctx.enter_context(tc.psum_pool(name="ps", bufs=1))

        offsets = sb.tile([P, J // 16], U16, name="offsets")
        x_scale_win = sb.tile([P, PASSES, T], U8, name="x_scale_win", align_bytes=64)
        x_win = [shared.tile([P, T], U32, name="x_win0", offset=0, align_bytes=64)]
        ga_col = sb.tile([P, 4], F32, name="ga_col")
        ident = sb.tile([P, P], F32, name="ident")
        warm = sb.tile([P, 8], F32, name="warm", tag="then_x1", align_bytes=64)
        warm_out = sb.tile([P, 8], F32, name="warm_out", tag="then_wb", align_bytes=64)

        nc.gpsimd.memset(warm[:], 0.0)
        nc.vector.memset(x_scale_win[:].bitcast(I32), 0)
        wb_scale = sb.tile([P, PASSES, N], U8, name="wb_scale", align_bytes=64)
        nc.gpsimd.memset(wb_scale[:].bitcast(I32), 0)
        nc.scalar.activation(warm_out[:], warm[:], ACT.Silu)

        def load_scales(eng, plane, rows):
            src = rows.bitcast(I32).rearrange("z (Q r) c -> r Q z c", r=4)
            for r in range(4):
                eng[r].dma_start(plane[:].bitcast(I32)[r:P:32, :, :], src[r])

        def load_words(z):
            nc.sync.dma_start(x_win[z][:].bitcast(I32), xt_words[z].rearrange("p c r -> p (c r)").bitcast(I32))

        wa_rows = wa.rearrange("(z p r) n -> z p r n", z=PASSES, r=4)

        nc.sync.dma_start(offsets[:], offs)
        nc.sync.dma_start(ga_col[:], ga.rearrange("o (p c) -> p (o c)", c=4))
        load_words(0)
        load_scales([nc.sync] * 4, x_scale_win, xt_scales)
        wb_code = sb.tile([P, PASSES, 2 * N], U8, name="wb_code", tag="then_wb", align_bytes=64)
        nc.sync.dma_start(wb_code[:].bitcast(I32), wb_words.rearrange("z p c -> p z c").bitcast(I32))
        x_win.append(sb.tile([P, T], U32, name="x_win1", tag="then_x1", align_bytes=64))
        load_words(1)
        load_scales([nc.sync, nc.gpsimd, nc.gpsimd, nc.gpsimd], wb_scale, wb_scales)

        make_identity(nc, ident[:])
        ga_ps = ps.tile([P, 4, P], F32, name="ga_ps", tag="e3")
        for c in range(4):
            nc.tensor.transpose(ga_ps[:, c, :], ga_col[:, c:c + 1].to_broadcast([P, P]), ident[:])
        raw = {}

        def load_wa(tile, at, z, m):
            raw[(z, m)] = tile[:, at * 4 * P:(at + 1) * 4 * P].rearrange("p (r n) -> p r n", r=4)
            nc.sync.dma_start(raw[(z, m)], wa_rows[z][:, :, m * P:(m + 1) * P])

        ga_all = sb.tile([P, J], F32, name="ga_all")
        nc.scalar.copy(ga_all[:].rearrange("p (n c) -> p n c", c=4), ga_ps[:].rearrange("p c n -> p n c"))

        x_code = [sb.tile([P, J], U32, name=f"x_code{z}", align_bytes=64) for z in range(PASSES)]
        x_scale = [shared.tile([P, J], U8, name=f"x_scale{z}", offset=z * J, align_bytes=64) for z in range(PASSES)]

        def gather_scales(z):
            nc.vector.tensor_copy(x_scale[z][:], x_scale_win[:, z, :].indirect(offsets[:]))

        def gather_words(z):
            nc.vector.tensor_copy(x_code[z][:], x_win[z][:].indirect(offsets[:]))

        wa_q = {}

        def cast(eng, raw, width, name):
            grouped = sb.tile([P, width, 4], BF16, name="g" + name, align_bytes=64)
            dst = grouped[:].rearrange("p (c i) r -> p c r i", i=4)
            src = raw.rearrange("p r (c i) -> p c r i", i=4)
            if eng is nc.scalar:
                nc.scalar.activation(dst, src, ACT.Copy, scale=-1.0)
            else:
                eng.tensor_scalar(dst, src, -1.0, 0.0, ALU.mult, ALU.add)
            return grouped

        def quantise(grouped, width, name, z, m0):
            code = sb.tile([P, width], U32, name="c" + name, align_bytes=64)
            scale = sb.tile([P, width], U8, name="s" + name, align_bytes=64)
            nc.vector.quantize_mx(code[:].bitcast(FP8X4), scale[:], grouped[:].rearrange("p n r -> p (n r)"))
            for i in range(width // P):
                wa_q[(z, m0 + i)] = (code[:, i * P:(i + 1) * P], scale[:, i * P:(i + 1) * P])

        b_ps = [ps.tile([P, J], F32, name=f"b{m}", tag=f"b{m}") for m in range(TILES)]
        e_ps = [ps.tile([P, J], F32, name=f"e{m}", tag=f"e{m}") for m in range(TILES)]

        def mm_b(dst, z, m, start, stop):
            nc.tensor.matmul_mx(dst[:], lhsT=wb_code[:, z, 2 * m * P:2 * (m + 1) * P].bitcast(FP4X4),
                                lhsT_scale=wb_scale[:, z, m * P:(m + 1) * P],
                                rhs=x_code[z][:].bitcast(FP8X4), rhs_scale=x_scale[z][:], start=start, stop=stop)

        def mm_a(z, m, start, stop):
            code, scale = wa_q[(z, m)]
            nc.tensor.matmul_mx(e_ps[m][:], lhsT=code.bitcast(FP8X4), lhsT_scale=scale,
                                rhs=x_code[z][:].bitcast(FP8X4), rhs_scale=x_scale[z][:], start=start, stop=stop)

        gather_words(0)
        gather_scales(0)
        raw_rest = shared.tile([P, 4 * 1024], F32, name="raw_rest", offset=PASSES * J, align_bytes=64)
        for m in range(TILES):
            for z in range(PASSES):
                load_wa(raw_rest, PASSES * m + z, z, m)
        gather_scales(1)
        for m in range(TILES):
            if m >= SPLIT_TILES:
                mm_b(e_ps[m], 0, m, True, False)
            mm_b(b_ps[m], 0, m, True, False)
        gather_words(1)

        b_sb = [sb.tile([P, J], F32, name=f"b_sb{m}") for m in range(SPLIT_TILES)]
        e_sb = [sb.tile([P, J], F32, name=f"e_sb{m}") for m in range(SPLIT_TILES)]
        s = [sb.tile([P, J], F32, name=f"s{m}") for m in range(TILES)]
        t = [sb.tile([P, J], F32, name=f"t{m}") for m in range(TILES)]
        y = [sb.tile([P, J], F32, name=f"y{m}") for m in range(TILES)]

        def sub(m):
            nc.vector.tensor_tensor(e_sb[m][:], e_ps[m][:], b_sb[m][:], ALU.add)

        def silu(m, cols=slice(0, J)):
            src = e_sb[m] if m < SPLIT_TILES else e_ps[m]
            nc.scalar.activation(s[m][:, cols], src[:, cols], ACT.Silu, scale=-0.5)

        def blend(m, cols=slice(0, J)):
            nc.vector.scalar_tensor_tensor(t[m][:, cols], s[m][:, cols], 2.0, b_ps[m][:, cols], ALU.mult, ALU.add)

        def gate(eng, m, cols=slice(0, J)):
            eng.tensor_tensor(y[m][:, cols], t[m][:, cols], ga_all[:, cols], ALU.mult)
            nc.sync.dma_start(out[m * P:(m + 1) * P, cols], y[m][:, cols])

        def products(m):
            if m >= SPLIT_TILES:
                mm_b(e_ps[m], 1, m, False, False)
            mm_b(b_ps[m], 1, m, False, True)
            for z, eng in enumerate((nc.scalar, nc.vector)):
                quantise(cast(eng, raw[(z, m)], P, f"{z}_{m}"), P, f"{z}_{m}", z, m)
            for z in range(PASSES):
                mm_a(z, m, z == 0 and m < SPLIT_TILES, z == 1)
            if m < SPLIT_TILES:
                nc.scalar.copy(b_sb[m][:], b_ps[m][:])

        def finish(m):
            pieces = (slice(0, J // 2), slice(J // 2, J)) if m == TILES - 1 else (slice(0, J),)
            if m < SPLIT_TILES:
                sub(m)
            for cols in pieces:
                silu(m, cols)
            for cols in pieces:
                blend(m, cols)
            for cols in pieces:
                gate(nc.gpsimd if m < SPLIT_TILES else nc.vector, m, cols)

        for step in range(TILES + 1):
            if step < TILES:
                products(step)
            if step >= 1:
                finish(step - 1)
